import numpy as np
CORES = [0,1,2,3,4,5,6,7]
N = 8
GROUPS = [[0,1,2,3],[4,5,6,7]]
def setup_inputs(rng):
    return {"x": rng.standard_normal((N, 128, 256), dtype=np.float32)}
def reference(x):
    y = np.empty((N, 128, 256), x.dtype)
    for g in GROUPS:
        s = x[g].max(axis=0)
        for r in g:
            y[r] = s
    return {"y": y}

@@ -1,0 +1,58 @@
+from concourse.bass import DstId, RemoteDMATransfer
+
+SHARDS = 4
+SCRATCH = {
+    "xs": ("dram", [SHARDS, 128, 64], "float32"),
+    "inb": ("dram", [SHARDS, 128, 64], "float32"),
+    "res": ("dram", [SHARDS, 128, 64], "float32"),
+}
+SEMAPHORES = ["loaded", "arr", "res0", "res1", "res2", "res3", "sent", "stored"]
+MAX = 2
+ALL = 0xFFFF
+
+
+def rank_program(g, core, T, topo):
+    rank = T.rank_of(core)
+    if rank is None:
+        return
+    group = [grp for grp in T.tables["GROUPS"] if rank in grp][0]
+    members = [T.cores[r] for r in group]
+    n = len(members)
+    k = group.index(rank)
+    others = [j for j in range(n) if j != k]
+
+    def dst(j):
+        rid, pid, _se = topo.addr(members[j])
+        return DstId(rid=rid, pnc=pid)
+
+    g.dma_start(T.xs[:], T.x[:]).then_inc(T.sem.loaded, 16)
+    g.wait_ge(T.sem.loaded, 16)
+
+    for j in others:
+        rid, pid, _se = topo.addr(members[j])
+        g.remote_dma(T.inb[k], T.xs[j], T.sem.arr, T.sem.sent, pid, rid, ALL)
+
+    g.wait_ge(T.sem.arr, 16 * (n - 1))
+    g.remote_dma_fused(
+        [RemoteDMATransfer(
+            dst_ids=[dst(j) for j in others],
+            dma_engine_mask=ALL,
+            remote_sem=T.sem["res%d" % k],
+            srcs=[T.xs[k]] + [T.inb[j] for j in others],
+            dsts=[T.res[k] for j in others],
+            alu_op=MAX,
+        )],
+        local_sem=T.sem.sent,
+    )
+
+    p = (k - 1) % n
+    g.wait_ge(T.sem["res%d" % p], 16)
+    rid, pid, _se = topo.addr(members[p])
+    g.remote_dma(T.res[p], T.res[p], T.sem["res%d" % p], T.sem.sent, pid, rid, ALL)
+
+    for j in range(n):
+        if j != p:
+            g.wait_ge(T.sem["res%d" % j], 16)
+    g.dma_start(T.y[:], T.res[:]).then_inc(T.sem.stored, 16)
+    g.wait_ge(T.sem.sent, 16 * (n - 1) + 16 + 16)
+    g.wait_ge(T.sem.stored, 16)

@@ -6,53 +6,53 @@ SCRATCH = {
     "inb": ("dram", [SHARDS, 128, 64], "float32"),
     "res": ("dram", [SHARDS, 128, 64], "float32"),
 }
-SEMAPHORES = ["loaded", "arr", "res0", "res1", "res2", "res3", "sent", "stored"]
+SEMAPHORES = ["loaded", "arr", "res", "sent", "stored"]
 MAX = 2
-ALL = 0xFFFF
 
 
 def rank_program(g, core, T, topo):
     rank = T.rank_of(core)
     if rank is None:
         return
-    group = [grp for grp in T.tables["GROUPS"] if rank in grp][0]
-    members = [T.cores[r] for r in group]
-    n = len(members)
-    k = group.index(rank)
-    others = [j for j in range(n) if j != k]
+    groups = T.tables["GROUPS"]
+    gi = [i for i in range(len(groups)) if rank in groups[i]][0]
+    k = groups[gi].index(rank)
+    folders = [T.cores[r] for r in groups[(gi + 1) % len(groups)]]
+    served = [T.cores[r] for r in groups[(gi - 1) % len(groups)]]
+    n = len(served)
 
-    def dst(j):
-        rid, pid, _se = topo.addr(members[j])
+    def dst(c):
+        rid, pid, _se = topo.addr(c)
         return DstId(rid=rid, pnc=pid)
 
-    g.dma_start(T.xs[:], T.x[:]).then_inc(T.sem.loaded, 16)
+    g.sync.dma_start(T.xs[:], T.x[:]).then_inc(T.sem.loaded, 16)
     g.wait_ge(T.sem.loaded, 16)
 
-    for j in others:
-        rid, pid, _se = topo.addr(members[j])
-        g.remote_dma(T.inb[k], T.xs[j], T.sem.arr, T.sem.sent, pid, rid, ALL)
-
-    g.wait_ge(T.sem.arr, 16 * (n - 1))
     g.remote_dma_fused(
         [RemoteDMATransfer(
-            dst_ids=[dst(j) for j in others],
-            dma_engine_mask=ALL,
-            remote_sem=T.sem["res%d" % k],
-            srcs=[T.xs[k]] + [T.inb[j] for j in others],
-            dsts=[T.res[k] for j in others],
+            dst_ids=[dst(folders[j])],
+            dma_engine_mask=0xF << (4 * j),
+            remote_sem=T.sem.arr,
+            src=T.xs[j],
+            dst=T.inb[k],
+        ) for j in range(n)],
+        local_sem=T.sem.sent,
+    )
+
+    g.wait_ge(T.sem.arr, 4 * n)
+    g.remote_dma_fused(
+        [RemoteDMATransfer(
+            dst_ids=[dst(c) for c in served],
+            dma_engine_mask=0xFFFF,
+            remote_sem=T.sem.res,
+            srcs=[T.inb[s] for s in range(n)],
+            dsts=[T.res[k] for c in served],
             alu_op=MAX,
         )],
         local_sem=T.sem.sent,
     )
 
-    p = (k - 1) % n
-    g.wait_ge(T.sem["res%d" % p], 16)
-    rid, pid, _se = topo.addr(members[p])
-    g.remote_dma(T.res[p], T.res[p], T.sem["res%d" % p], T.sem.sent, pid, rid, ALL)
-
-    for j in range(n):
-        if j != p:
-            g.wait_ge(T.sem["res%d" % j], 16)
-    g.dma_start(T.y[:], T.res[:]).then_inc(T.sem.stored, 16)
-    g.wait_ge(T.sem.sent, 16 * (n - 1) + 16 + 16)
-    g.wait_ge(T.sem.stored, 16)
+    g.sync.wait_ge(T.sem.res, 16 * n)
+    g.sync.dma_start(T.y[:], T.res[:]).then_inc(T.sem.stored, 16)
+    g.sync.wait_ge(T.sem.stored, 16)
+    g.wait_ge(T.sem.sent, 4 * n + 16)

from concourse.bass import DstId, RemoteDMATransfer

SHARDS = 4
SCRATCH = {
    "xs": ("dram", [SHARDS, 128, 64], "float32"),
    "inb": ("dram", [SHARDS, 128, 64], "float32"),
    "res": ("dram", [SHARDS, 128, 64], "float32"),
}
SEMAPHORES = ["loaded", "arr", "res", "sent", "stored"]
MAX = 2


def rank_program(g, core, T, topo):
    rank = T.rank_of(core)
    if rank is None:
        return
    groups = T.tables["GROUPS"]
    gi = [i for i in range(len(groups)) if rank in groups[i]][0]
    k = groups[gi].index(rank)
    folders = [T.cores[r] for r in groups[(gi + 1) % len(groups)]]
    served = [T.cores[r] for r in groups[(gi - 1) % len(groups)]]
    n = len(served)

    def dst(c):
        rid, pid, _se = topo.addr(c)
        return DstId(rid=rid, pnc=pid)

    g.sync.dma_start(T.xs[:], T.x[:]).then_inc(T.sem.loaded, 16)
    g.wait_ge(T.sem.loaded, 16)

    g.remote_dma_fused(
        [RemoteDMATransfer(
            dst_ids=[dst(folders[j])],
            dma_engine_mask=0xF << (4 * j),
            remote_sem=T.sem.arr,
            src=T.xs[j],
            dst=T.inb[k],
        ) for j in range(n)],
        local_sem=T.sem.sent,
    )

    g.wait_ge(T.sem.arr, 4 * n)
    g.remote_dma_fused(
        [RemoteDMATransfer(
            dst_ids=[dst(c) for c in served],
            dma_engine_mask=0xFFFF,
            remote_sem=T.sem.res,
            srcs=[T.inb[s] for s in range(n)],
            dsts=[T.res[k] for c in served],
            alu_op=MAX,
        )],
        local_sem=T.sem.sent,
    )

    g.sync.wait_ge(T.sem.res, 16 * n)
    g.sync.dma_start(T.y[:], T.res[:]).then_inc(T.sem.stored, 16)
    g.sync.wait_ge(T.sem.stored, 16)
    g.wait_ge(T.sem.sent, 4 * n + 16)
